import numpy as np
import ml_dtypes


def mxq(x, axis, fmt="e4m3"):
    dtype, down = {"e4m3": (ml_dtypes.float8_e4m3fn, 7), "e5m2": (ml_dtypes.float8_e5m2, 14)}[fmt]
    v = np.moveaxis(np.asarray(x, np.float32).astype(ml_dtypes.bfloat16).astype(np.float64), axis, -1)
    blocks = v.reshape(v.shape[:-1] + (-1, 32))
    amax = np.abs(blocks).max(-1, keepdims=True)
    byte = np.maximum(np.where(amax > 0, np.frexp(amax)[1] - 1 + 127, 0) - down, 1)
    scale = np.exp2(byte - 127.0)
    codes = (blocks / scale).astype(np.float32).astype(dtype).astype(np.float64)
    return np.moveaxis((codes * scale).reshape(v.shape), -1, axis)


WIDE = False


def mx_kscale(k):
    if not WIDE:
        return np.ones(k)
    levels = np.array([10, -10, 5, -5, 0])
    if k % 512:
        return np.exp2(np.random.permutation(np.resize(levels, k // 32))).repeat(32)
    a = np.empty((k // 512, 16))
    for p in range(k // 512):
        a[p, :8] = np.random.permutation(np.resize(levels, 8))
        for g in range(8):
            far = levels[np.abs(levels - a[p, g]) >= 10]
            a[p, g + 8] = far[np.random.randint(len(far))]
    return np.exp2(a.ravel()).repeat(32)


def f64(x):
    return np.asarray(x).astype(np.float64)


def striped(idx):
    return np.tile(np.asarray(idx).reshape(-1, 16).T, (8, 1)).astype(np.uint16)


def unstriped(offs):
    return offs[:16].T.reshape(-1).astype(np.int64)


E2M1 = np.array([0.0, 0.5, 1.0, 1.5, 2.0, 3.0, 4.0, 6.0, -0.0, -0.5, -1.0, -1.5, -2.0, -3.0, -4.0, -6.0])


def pack_weight(w, fmt):
    k, n = w.shape
    w = f64(np.asarray(w, np.float32).astype(ml_dtypes.bfloat16)).reshape(k // 32, 32, n)
    amax = np.abs(w).max(1)
    if fmt == "e4m3":
        byte = np.frexp(amax)[1] - 1 + 127 - 7
    else:
        mant, ex = np.frexp(amax / 6.0)
        byte = np.where(mant > 0.5, ex, ex - 1) + 127
    byte = np.clip(np.where(amax > 0, byte, 1), 1, 254)
    scaled = (w * np.exp2(127.0 - byte)[:, None, :]).reshape(k, n).astype(np.float32)
    by_word = np.ascontiguousarray(scaled.reshape(k // 512, 128, 4, n).transpose(0, 1, 3, 2))
    if fmt == "e4m3":
        words = by_word.astype(ml_dtypes.float8_e4m3fn).view(np.uint8)
    else:
        c = by_word.astype(ml_dtypes.float4_e2m1fn).view(np.uint8) & 0xF
        words = (c[..., 0::2] | (c[..., 1::2] << 4)).reshape(k // 512, 128, 2 * n)
    return np.ascontiguousarray(words), np.ascontiguousarray(byte.astype(np.uint8).reshape(k // 512, 16, n))


def unpack_weight(words, scales, fmt):
    g, _, n = scales.shape
    words = np.ascontiguousarray(words).reshape(g, 128, n, -1)
    if fmt == "e4m3":
        vals = words.view(ml_dtypes.float8_e4m3fn).astype(np.float64)
    else:
        nib = np.empty((g, 128, n, 4), np.uint8)
        nib[..., 0::2] = words & 0xF
        nib[..., 1::2] = words >> 4
        vals = E2M1[nib]
    vals = vals * np.repeat(np.exp2(scales.astype(np.float64) - 127.0), 8, axis=1)[..., None]
    return vals.transpose(0, 1, 3, 2).reshape(g * 512, n)


def bf(x):
    return np.asarray(x, np.float32).astype(ml_dtypes.bfloat16)


def planes(Y):
    r, m = Y.shape
    b = f64(bf(Y)).reshape(r // 32, 32, m)
    amax = np.abs(b).max(1)
    byte = np.clip(np.where(amax > 0, np.frexp(amax)[1] - 1 + 127 - 7, 1), 1, 254)
    codes = (b * np.exp2(127.0 - byte)[:, None, :]).reshape(r, m).astype(np.float32).astype(ml_dtypes.float8_e4m3fn).view(np.uint8)
    words = codes.reshape(r // 512, 128, 4, m).transpose(0, 1, 3, 2)
    return np.ascontiguousarray(words), np.ascontiguousarray(byte.astype(np.uint8).reshape(r // 512, 16, m))


K, T, J, N, M = 1024, 1024, 512, 512, 512


def setup_inputs():
    n = np.random.standard_normal
    idx = np.random.permutation(T)[:J]
    fk = mx_kscale(K)
    ft = mx_kscale(T)
    xtp = pack_weight(n((K, J)) / fk[:, None], "e2m1")
    wp = pack_weight(n((K, N)) * 1 / np.sqrt(K) * fk[:, None], "e4m3")
    kyp = pack_weight(n((T, M)) * 1 / np.sqrt(T) * ft[:, None], "e2m1")
    return {
        "xt_words": xtp[0],
        "xt_scales": xtp[1],
        "w_words": wp[0],
        "w_scales": wp[1],
        "old": (1.0 * n((N, T))).astype(np.float32),
        "ct1": (np.random.uniform(0.5, 2.0, (T, 1)) / ft[:, None]).astype(np.float32),
        "ky_words": kyp[0],
        "ky_scales": kyp[1],
        "offs": striped(idx),
    }


def reference(xt_words, xt_scales, w_words, w_scales, old, ct1, ky_words, ky_scales, offs):
    idx = unstriped(offs)
    xtu = unpack_weight(xt_words, xt_scales, "e2m1")
    wu = unpack_weight(w_words, w_scales, "e4m3")
    kyu = unpack_weight(ky_words, ky_scales, "e2m1")
    p = wu.T @ xtu
    pp = np.zeros((N, T))
    pp[:, idx] = p
    pg = pp + 0.5 * f64(old)
    pt = pg.T
    pw = pt * f64(ct1)
    pwq = mxq(pw, 0, "e4m3")
    y = pwq.T @ kyu
    words, scales = planes(y)
    return y, words, scales

@@ -1,0 +1,292 @@
+from contextlib import ExitStack
+
+import concourse.mybir as mybir
+from concourse.masks import make_identity
+
+K, T, J, N, M = 1024, 1024, 512, 512, 512
+FLOPS = 2 * K * N * J + 2 * T * N * M
+
+F32 = mybir.dt.float32
+BF16 = mybir.dt.bfloat16
+I32 = mybir.dt.int32
+U32 = mybir.dt.uint32
+U16 = mybir.dt.uint16
+U8 = mybir.dt.uint8
+FP8X4 = mybir.dt.float8_e4m3fn_x4
+FP4X4 = mybir.dt.float4_e2m1fn_x4
+COPY = mybir.ActivationFunctionType.Copy
+ADD = mybir.AluOpType.add
+MULT = mybir.AluOpType.mult
+
+P = 128
+PACK = 4
+PASS = P * PACK
+PASSES = 2
+FIRST_PIECES = (128, 128, 256,)
+ON_TENSOR = ((0, 0), (0, 1), (1, 0), (1, 1))
+CHUNK = 128
+HALF = 256
+
+
+def load_scales(nc, queue, plane, scales, rows):
+    for r in rows:
+        queue.dma_start(
+            out=plane[r:P:32, :, :].bitcast(I32),
+            in_=scales[:, r:16:4, :].rearrange("z q c -> q z c").bitcast(I32),
+        )
+
+
+def tile_moe_expert_page_to_keys_pl_kernel(
+    tc, xt_words, xt_scales, w_words, w_scales, old, ct1, ky_words, ky_scales, offs, out_0, out_1, out_2
+):
+    nc = tc.nc
+    with ExitStack() as ctx:
+        keep = ctx.enter_context(tc.tile_pool(name="keep", bufs=1))
+        ring = ctx.enter_context(tc.tile_pool(name="ring", bufs=2))
+        loads = ctx.enter_context(tc.tile_pool(name="loads", bufs=1))
+        psum = ctx.enter_context(tc.psum_pool(name="psum", bufs=8))
+
+        offsets = keep.tile([P, J // 16], U16, name="offsets")
+        ws_raw = loads.tile([P, PASSES, N], U8, name="ws_raw", align_bytes=64, offset=4032)
+        xs = keep.tile([P, PASSES, J], U8, name="xs", align_bytes=64)
+        ks = loads.tile([P, PASSES, M], U8, name="ks", align_bytes=64, offset=15360)
+        w_raw = loads.tile([P, PASSES, N], I32, name="w_raw", align_bytes=64, offset=13248)
+        xw = keep.tile([P, PASSES, 2 * J], U8, name="xw", align_bytes=64)
+        kw = loads.tile([P, PASSES, 2 * M], U8, name="kw", align_bytes=64, offset=13312)
+        w_dealt = [keep.tile([P, PASSES, P], I32, name="w_first", align_bytes=64),
+                   keep.tile([P, PACK - 1, PASSES, P], I32, name="w_rest", align_bytes=64)]
+        ws = keep.tile([P, PACK, PASSES, P], U8, name="ws", align_bytes=64)
+        ct = loads.tile([P, PASSES, PACK], F32, name="ct", offset=4096)
+        ct_half = keep.tile([P, PASSES, PACK], F32, name="ct_half")
+        ident = keep.tile([P, P], F32, name="ident")
+        olds = [loads.tile([P, T], F32, name=f"old{r}", offset=at) for r, at in enumerate((0, 5024, 9216, 0))]
+        windows = [keep.tile([P, T], F32, name="window0"), loads.tile([P, T], F32, name="window1", offset=17280)]
+        y_early = keep.tile([P, 2, M], F32, name="y_early")
+        y_late = keep.tile([P, M // CHUNK, 2, CHUNK], F32, name="y_late")
+        rounded = keep.tile([P, M, PACK], BF16, name="rounded", align_bytes=64)
+        y_scales = keep.tile([P, M], U8, name="y_scales", align_bytes=64)
+
+        nc.vector.memset(ws_raw[:].rearrange("p z c -> p (z c)").bitcast(I32), 0)
+        nc.vector.memset(xs[:].rearrange("p z c -> p (z c)").bitcast(I32), 0)
+        nc.sync.dma_start(offsets[:], offs)
+        nc.sync.dma_start(out=xw[:].bitcast(I32), in_=xt_words.rearrange("z p c -> p z c").bitcast(I32))
+        load_scales(nc, nc.sync, ws_raw, w_scales, range(4))
+        nc.sync.dma_start(out=w_raw[:], in_=w_words.rearrange("z p n t -> p z (n t)").bitcast(I32))
+        load_scales(nc, nc.sync, xs, xt_scales, range(4))
+        make_identity(nc, ident[:])
+        nc.vector.memset(windows[0][:], 0.0)
+
+        nc.vector.tensor_copy(
+            out=ws[:].rearrange("p r z q -> p z q r"),
+            in_=ws_raw[:].rearrange("p z (q r) -> p z q r", r=PACK),
+        )
+        w_cols = w_raw[:].rearrange("p z (q r) -> p z q r", r=PACK)
+        nc.vector.tensor_copy(out=w_dealt[0][:], in_=w_cols[:, :, :, 0])
+        nc.vector.tensor_copy(out=w_dealt[1][:].rearrange("p r z q -> p z q r"), in_=w_cols[:, :, :, 1:PACK])
+
+        old_rows = old.rearrange("(p r) t -> p r t", r=PACK)
+        nc.sync.dma_start(out=olds[0][:], in_=old_rows[:, 0, :])
+        nc.sync.dma_start(out=ct[:], in_=ct1.rearrange("(g p r) o -> p g (r o)", g=PASSES, r=PACK))
+        nc.sync.dma_start(out=olds[1][:], in_=old_rows[:, 1, :])
+        nc.gpsimd.memset(ks[:].rearrange("p z c -> p (z c)").bitcast(I32), 0)
+        nc.gpsimd.memset(windows[1][:], 0.0)
+        nc.sync.dma_start(out=kw[:].bitcast(I32), in_=ky_words.rearrange("z p c -> p z c").bitcast(I32))
+        load_scales(nc, nc.sync, ks, ky_scales, range(4))
+        nc.sync.dma_start(out=olds[2][:], in_=old_rows[:, 2, :])
+
+        def w_block(r, z):
+            words = w_dealt[0][:, z, :] if r == 0 else w_dealt[1][:, r - 1, z, :]
+            return words.bitcast(FP8X4)
+
+        def expert(r, j0, width):
+            acc = psum.tile([P, J], F32, name="bank", tag="bank")
+            step = J if width == J else CHUNK
+            for c in range(0, width, step):
+                for z in range(PASSES):
+                    nc.tensor.matmul_mx(
+                        out=acc[:, c : c + step],
+                        lhsT=w_block(r, z),
+                        lhsT_scale=ws[:, r, z, :],
+                        rhs=xw[:, z, 2 * (j0 + c) : 2 * (j0 + c + step)].bitcast(FP4X4),
+                        rhs_scale=xs[:, z, j0 + c : j0 + c + step],
+                        start=(z == 0),
+                        stop=(z == PASSES - 1),
+                    )
+            return acc
+
+        def double(acc, c0, width, tag):
+            doubled = keep.tile([P, width], F32, name="doubled", tag=tag)
+            nc.scalar.activation(out=doubled[:], in_=acc[:, c0 : c0 + width], func=COPY, scale=2.0)
+            return doubled
+
+        def scatter(r, j0, doubled):
+            width = doubled.shape[1]
+            window = windows[r % 2]
+            nc.vector.tensor_copy(window[:].indirect(offsets[:, j0 // 16 : (j0 + width) // 16]), doubled[:])
+
+        def deal_old(r, g):
+            dealt = keep.tile([P, PACK, P], F32, name=f"old_dealt{r}_{g}")
+            nc.scalar.copy(
+                out=dealt[:].rearrange("p s (c i) -> p c s i", i=4),
+                in_=olds[r][:, g * PASS : (g + 1) * PASS].rearrange("p (c i s) -> p c s i", i=4, s=PACK),
+            )
+            return dealt
+
+        def turn_adding_on_tensor(r, g, dealt):
+            bank = psum.tile([P, PACK, P], F32, name="bank", tag="bank")
+            for s in range(PACK):
+                cols = windows[r % 2][:, g * PASS + s : (g + 1) * PASS : PACK]
+                nc.tensor.matmul(bank[:, s, :], cols, ident[:], start=(s == 0), stop=False, is_transpose=True)
+            for s in range(PACK):
+                nc.tensor.matmul(bank[:, s, :], dealt[:, s, :], ident[:], start=False, stop=(s == PACK - 1), is_transpose=True)
+            return bank
+
+        def turn_adding_on_vector(r, g):
+            cols = slice(g * PASS, (g + 1) * PASS)
+            page = ring.tile([P, PACK, P], F32, name="page", tag=f"page{g}")
+            nc.vector.tensor_tensor(
+                out=page[:].rearrange("p s q -> p q s"),
+                in0=windows[r % 2][:, cols].rearrange("p (q s) -> p q s", s=PACK),
+                in1=olds[r][:, cols].rearrange("p (q s) -> p q s", s=PACK),
+                op=ADD,
+            )
+            bank = psum.tile([P, PACK, P], F32, name="bank", tag="bank")
+            for s in range(PACK):
+                nc.tensor.transpose(bank[:, s, :], page[:, s, :], ident[:])
+            return bank
+
+        def weigh_on_scalar(r, bank, g, grouped):
+            flat = keep.tile([P, PACK, P], BF16, name="flat", tag=f"flat{r}_{g}")
+            for s in range(PACK):
+                nc.scalar.activation(out=flat[:, s, :], in_=bank[:, s, :], func=COPY, scale=ct_half[:, g, s : s + 1])
+            nc.scalar.copy(
+                out=grouped.rearrange("p (c i s) -> p c s i", i=4, s=PACK),
+                in_=flat[:].rearrange("p s (c i) -> p c s i", i=4),
+            )
+
+        def weigh_on_vector(bank, g, grouped):
+            nc.vector.tensor_tensor(
+                out=grouped.rearrange("p (n s) -> p n s", s=PACK),
+                in0=bank[:].rearrange("p s n -> p n s"),
+                in1=ct_half[:, g, :].unsqueeze(1).to_broadcast([P, P, PACK]),
+                op=MULT,
+            )
+
+        out_rows = out_0.rearrange("(p r) m -> p r m", r=PACK)
+
+        def keys(codes, scales, g, acc, m0, width):
+            nc.tensor.matmul_mx(
+                out=acc,
+                lhsT=codes.bitcast(FP8X4),
+                lhsT_scale=scales,
+                rhs=kw[:, g, 2 * m0 : 2 * (m0 + width)].bitcast(FP4X4),
+                rhs_scale=ks[:, g, m0 : m0 + width],
+                start=(g == 0),
+                stop=(g == PASSES - 1),
+            )
+
+        def front(r):
+            grouped = keep.tile([P, T], BF16, name=f"grouped{r}", align_bytes=64)
+            for g in range(PASSES):
+                if (r, g) in dealt:
+                    bank = turn_adding_on_tensor(r, g, dealt[r, g])
+                else:
+                    bank = turn_adding_on_vector(r, g)
+                weigh_on_scalar(r, bank, g, grouped[:, g * PASS : (g + 1) * PASS])
+            return grouped
+
+        def back(r, grouped):
+            codes = ring.tile([P, PASSES * P], U32, name="codes", tag="codes", align_bytes=64)
+            scales = ring.tile([P, PASSES * P], U8, name="scales", tag="scales", align_bytes=64)
+            nc.vector.quantize_mx(out=codes[:].bitcast(FP8X4), scales=scales[:], in_=grouped[:])
+            acc = psum.tile([P, M], F32, name="bank", tag="bank")
+            for g in range(PASSES):
+                keys(codes[:, g * P : (g + 1) * P], scales[:, g * P : (g + 1) * P], g, acc[:], 0, M)
+            if r < 2:
+                nc.scalar.copy(out=y_early[:, r, :], in_=acc[:])
+                nc.sync.dma_start(out=out_rows[:, r, :], in_=y_early[:, r, :])
+            else:
+                nc.scalar.copy(out=y_late[:, :, 0, :], in_=acc[:].rearrange("p (c m) -> p c m", m=CHUNK))
+                nc.sync.dma_start(out=out_rows[:, r, :].rearrange("p (c m) -> p c m", m=CHUNK), in_=y_late[:, :, 0, :])
+
+        last = PACK - 1
+        firsts = []
+        j0 = 0
+        for width in FIRST_PIECES:
+            firsts.append((j0, double(expert(0, j0, width), 0, width, f"first{j0}")))
+            j0 = j0 + width
+        second = double(expert(1, 0, J), 0, J, "second")
+        late_accs = {r: expert(r, 0, J) for r in (2, last)}
+        late_heads = {r: double(late_accs[r], 0, HALF, f"head{r}") for r in (2, last)}
+        nc.gpsimd.tensor_scalar(out=ct_half[:], in0=ct[:], scalar1=0.5, scalar2=None, op0=MULT)
+        dealt = {(r, g): deal_old(r, g) for r, g in ON_TENSOR}
+        nc.sync.dma_start(out=olds[last][:], in_=old_rows[:, last, :])
+
+        for j0, doubled in firsts:
+            scatter(0, j0, doubled)
+        grouped0 = front(0)
+        scatter(1, 0, second)
+        grouped1 = front(1)
+        scatter(2, 0, late_heads[2])
+        rest = double(late_accs[2], HALF, HALF, "flat0_1")
+        back(0, grouped0)
+        scatter(2, HALF, rest)
+        grouped2 = front(2)
+        scatter(last, 0, late_heads[last])
+        rest = double(late_accs[last], HALF, HALF, "flat1_1")
+        back(1, grouped1)
+        nc.scalar.copy(out=rounded[:, :, 0:2], in_=y_early[:].rearrange("p r m -> p m r"))
+        scatter(last, HALF, rest)
+
+        banks = [turn_adding_on_vector(last, g) for g in range(PASSES)]
+        back(2, grouped2)
+        tails = [keep.tile([P, PASS], BF16, name=f"tail{g}", align_bytes=64) for g in range(PASSES)]
+        for g in range(PASSES):
+            weigh_on_vector(banks[g], g, tails[g][:, 0:PASS])
+        accs = [psum.tile([P, M], F32, name="bank", tag="bank") for c in range(M // CHUNK)]
+        for g in range(PASSES):
+            codes = keep.tile([P, P], U32, name=f"last_codes{g}", align_bytes=64)
+            scales = keep.tile([P, P], U8, name=f"last_scales{g}", align_bytes=64)
+            nc.vector.quantize_mx(out=codes[:].bitcast(FP8X4), scales=scales[:], in_=tails[g][:, 0:PASS])
+            for c in range(M // CHUNK):
+                keys(codes[:], scales[:], g, accs[c][:, 0:CHUNK], c * CHUNK, CHUNK)
+
+        y_codes = keep.tile([P, M], U32, name="y_codes", align_bytes=64)
+        words_out = out_1[0].rearrange("p c t -> p (c t)")
+
+        def finish(c):
+            cols = slice(c * CHUNK, (c + 1) * CHUNK)
+            nc.scalar.copy(out=y_late[:, c, 1, :], in_=accs[c][:, 0:CHUNK])
+            nc.vector.tensor_copy(out=rounded[:, cols, 2:4], in_=y_late[:, c, :, :].rearrange("p r m -> p m r"))
+
+        def planes(m0, m1):
+            nc.vector.quantize_mx(
+                out=y_codes[:, m0:m1].bitcast(FP8X4),
+                scales=y_scales[:, m0:m1],
+                in_=rounded[:, m0:m1, :].rearrange("p m r -> p (m r)"),
+            )
+
+        def store(h):
+            cols = slice(h * HALF, (h + 1) * HALF)
+            nc.scalar.dma_start(
+                out=out_rows[:, last, cols].rearrange("p (c m) -> p c m", m=CHUNK), in_=y_late[:, 2 * h : 2 * h + 2, 1, :]
+            )
+            nc.sync.dma_start(
+                out=words_out[:, h * HALF * PACK : (h + 1) * HALF * PACK].bitcast(I32), in_=y_codes[:, cols].bitcast(I32)
+            )
+
+        finish(0)
+        finish(1)
+        finish(2)
+        planes(0, HALF)
+        finish(3)
+        planes(HALF, HALF + CHUNK)
+        planes(HALF + CHUNK, M)
+        store(0)
+        store(1)
+        for quad in range(4):
+            queue = nc.sync if quad % 2 == 0 else nc.scalar
+            queue.dma_start(
+                out=out_2[0, 4 * quad : 4 * quad + 4, :].bitcast(I32),
+                in_=y_scales[32 * quad : 32 * quad + 4, :].bitcast(I32),
+            )

@@ -22,8 +22,8 @@ P = 128
 PACK = 4
 PASS = P * PACK
 PASSES = 2
-FIRST_PIECES = (128, 128, 256,)
-ON_TENSOR = ((0, 0), (0, 1), (1, 0), (1, 1))
+FIRST_PIECES = (128, 384)
+HEAD2 = 384
 CHUNK = 128
 HALF = 256
 
@@ -43,6 +43,7 @@ def tile_moe_expert_page_to_keys_pl_kernel(
     with ExitStack() as ctx:
         keep = ctx.enter_context(tc.tile_pool(name="keep", bufs=1))
         ring = ctx.enter_context(tc.tile_pool(name="ring", bufs=2))
+        late = ctx.enter_context(tc.tile_pool(name="late", bufs=1))
         loads = ctx.enter_context(tc.tile_pool(name="loads", bufs=1))
         psum = ctx.enter_context(tc.psum_pool(name="psum", bufs=8))
 
@@ -53,16 +54,14 @@ def tile_moe_expert_page_to_keys_pl_kernel(
         w_raw = loads.tile([P, PASSES, N], I32, name="w_raw", align_bytes=64, offset=13248)
         xw = keep.tile([P, PASSES, 2 * J], U8, name="xw", align_bytes=64)
         kw = loads.tile([P, PASSES, 2 * M], U8, name="kw", align_bytes=64, offset=13312)
-        w_dealt = [keep.tile([P, PASSES, P], I32, name="w_first", align_bytes=64),
-                   keep.tile([P, PACK - 1, PASSES, P], I32, name="w_rest", align_bytes=64)]
+        w_dealt = [keep.tile([P, 2, PASSES, P], I32, name=f"w_dealt{a}", align_bytes=64) for a in range(2)]
         ws = keep.tile([P, PACK, PASSES, P], U8, name="ws", align_bytes=64)
         ct = loads.tile([P, PASSES, PACK], F32, name="ct", offset=4096)
         ct_half = keep.tile([P, PASSES, PACK], F32, name="ct_half")
         ident = keep.tile([P, P], F32, name="ident")
         olds = [loads.tile([P, T], F32, name=f"old{r}", offset=at) for r, at in enumerate((0, 5024, 9216, 0))]
         windows = [keep.tile([P, T], F32, name="window0"), loads.tile([P, T], F32, name="window1", offset=17280)]
-        y_early = keep.tile([P, 2, M], F32, name="y_early")
-        y_late = keep.tile([P, M // CHUNK, 2, CHUNK], F32, name="y_late")
+        y = keep.tile([P, M // CHUNK, PACK, CHUNK], F32, name="y")
         rounded = keep.tile([P, M, PACK], BF16, name="rounded", align_bytes=64)
         y_scales = keep.tile([P, M], U8, name="y_scales", align_bytes=64)
 
@@ -80,9 +79,9 @@ def tile_moe_expert_page_to_keys_pl_kernel(
             out=ws[:].rearrange("p r z q -> p z q r"),
             in_=ws_raw[:].rearrange("p z (q r) -> p z q r", r=PACK),
         )
-        w_cols = w_raw[:].rearrange("p z (q r) -> p z q r", r=PACK)
-        nc.vector.tensor_copy(out=w_dealt[0][:], in_=w_cols[:, :, :, 0])
-        nc.vector.tensor_copy(out=w_dealt[1][:].rearrange("p r z q -> p z q r"), in_=w_cols[:, :, :, 1:PACK])
+        w_cols = w_raw[:].rearrange("p z (q a e) -> p a z q e", a=2, e=2)
+        for a in range(2):
+            nc.vector.tensor_copy(out=w_dealt[a][:].rearrange("p e z q -> p z q e"), in_=w_cols[:, a])
 
         old_rows = old.rearrange("(p r) t -> p r t", r=PACK)
         nc.sync.dma_start(out=olds[0][:], in_=old_rows[:, 0, :])
@@ -95,8 +94,7 @@ def tile_moe_expert_page_to_keys_pl_kernel(
         nc.sync.dma_start(out=olds[2][:], in_=old_rows[:, 2, :])
 
         def w_block(r, z):
-            words = w_dealt[0][:, z, :] if r == 0 else w_dealt[1][:, r - 1, z, :]
-            return words.bitcast(FP8X4)
+            return w_dealt[r // 2][:, r % 2, z, :].bitcast(FP8X4)
 
         def expert(r, j0, width):
             acc = psum.tile([P, J], F32, name="bank", tag="bank")
@@ -114,9 +112,8 @@ def tile_moe_expert_page_to_keys_pl_kernel(
                     )
             return acc
 
-        def double(acc, c0, width, tag):
-            doubled = keep.tile([P, width], F32, name="doubled", tag=tag)
-            nc.scalar.activation(out=doubled[:], in_=acc[:, c0 : c0 + width], func=COPY, scale=2.0)
+        def double(acc, c0, doubled):
+            nc.scalar.activation(out=doubled[:], in_=acc[:, c0 : c0 + doubled.shape[1]], func=COPY, scale=2.0)
             return doubled
 
         def scatter(r, j0, doubled):
@@ -127,27 +124,26 @@ def tile_moe_expert_page_to_keys_pl_kernel(
         def deal_old(r, g):
             dealt = keep.tile([P, PACK, P], F32, name=f"old_dealt{r}_{g}")
             nc.scalar.copy(
-                out=dealt[:].rearrange("p s (c i) -> p c s i", i=4),
-                in_=olds[r][:, g * PASS : (g + 1) * PASS].rearrange("p (c i s) -> p c s i", i=4, s=PACK),
+                out=dealt[:].rearrange("p (a e) q -> p a q e", e=2),
+                in_=olds[r][:, g * PASS : (g + 1) * PASS].rearrange("p (q a e) -> p a q e", a=2, e=2),
             )
             return dealt
 
         def turn_adding_on_tensor(r, g, dealt):
             bank = psum.tile([P, PACK, P], F32, name="bank", tag="bank")
             for s in range(PACK):
-                cols = windows[r % 2][:, g * PASS + s : (g + 1) * PASS : PACK]
-                nc.tensor.matmul(bank[:, s, :], cols, ident[:], start=(s == 0), stop=False, is_transpose=True)
+                nc.tensor.matmul(bank[:, s, :], dealt[:, s, :], ident[:], start=(s == 0), stop=False, is_transpose=True)
             for s in range(PACK):
-                nc.tensor.matmul(bank[:, s, :], dealt[:, s, :], ident[:], start=False, stop=(s == PACK - 1), is_transpose=True)
+                cols = windows[r % 2][:, g * PASS + s : (g + 1) * PASS : PACK]
+                nc.tensor.matmul(bank[:, s, :], cols, ident[:], start=False, stop=(s == PACK - 1), is_transpose=True)
             return bank
 
-        def turn_adding_on_vector(r, g):
+        def turn_adding_on_vector(r, g, page):
             cols = slice(g * PASS, (g + 1) * PASS)
-            page = ring.tile([P, PACK, P], F32, name="page", tag=f"page{g}")
             nc.vector.tensor_tensor(
-                out=page[:].rearrange("p s q -> p q s"),
-                in0=windows[r % 2][:, cols].rearrange("p (q s) -> p q s", s=PACK),
-                in1=olds[r][:, cols].rearrange("p (q s) -> p q s", s=PACK),
+                out=page[:].rearrange("p (a e) q -> p a q e", e=2),
+                in0=windows[r % 2][:, cols].rearrange("p (q a e) -> p a q e", a=2, e=2),
+                in1=olds[r][:, cols].rearrange("p (q a e) -> p a q e", a=2, e=2),
                 op=ADD,
             )
             bank = psum.tile([P, PACK, P], F32, name="bank", tag="bank")
@@ -155,8 +151,7 @@ def tile_moe_expert_page_to_keys_pl_kernel(
                 nc.tensor.transpose(bank[:, s, :], page[:, s, :], ident[:])
             return bank
 
-        def weigh_on_scalar(r, bank, g, grouped):
-            flat = keep.tile([P, PACK, P], BF16, name="flat", tag=f"flat{r}_{g}")
+        def weigh_on_scalar(bank, g, grouped, flat):
             for s in range(PACK):
                 nc.scalar.activation(out=flat[:, s, :], in_=bank[:, s, :], func=COPY, scale=ct_half[:, g, s : s + 1])
             nc.scalar.copy(
@@ -166,9 +161,9 @@ def tile_moe_expert_page_to_keys_pl_kernel(
 
         def weigh_on_vector(bank, g, grouped):
             nc.vector.tensor_tensor(
-                out=grouped.rearrange("p (n s) -> p n s", s=PACK),
-                in0=bank[:].rearrange("p s n -> p n s"),
-                in1=ct_half[:, g, :].unsqueeze(1).to_broadcast([P, P, PACK]),
+                out=grouped.rearrange("p (c e s) -> p c s e", e=2, s=PACK),
+                in0=bank[:].rearrange("p s (c e) -> p c s e", e=2),
+                in1=ct_half[:, g, :].unsqueeze(1).unsqueeze(3).to_broadcast([P, P // 2, PACK, 2]),
                 op=MULT,
             )
 
@@ -185,16 +180,6 @@ def tile_moe_expert_page_to_keys_pl_kernel(
                 stop=(g == PASSES - 1),
             )
 
-        def front(r):
-            grouped = keep.tile([P, T], BF16, name=f"grouped{r}", align_bytes=64)
-            for g in range(PASSES):
-                if (r, g) in dealt:
-                    bank = turn_adding_on_tensor(r, g, dealt[r, g])
-                else:
-                    bank = turn_adding_on_vector(r, g)
-                weigh_on_scalar(r, bank, g, grouped[:, g * PASS : (g + 1) * PASS])
-            return grouped
-
         def back(r, grouped):
             codes = ring.tile([P, PASSES * P], U32, name="codes", tag="codes", align_bytes=64)
             scales = ring.tile([P, PASSES * P], U8, name="scales", tag="scales", align_bytes=64)
@@ -202,44 +187,57 @@ def tile_moe_expert_page_to_keys_pl_kernel(
             acc = psum.tile([P, M], F32, name="bank", tag="bank")
             for g in range(PASSES):
                 keys(codes[:, g * P : (g + 1) * P], scales[:, g * P : (g + 1) * P], g, acc[:], 0, M)
-            if r < 2:
-                nc.scalar.copy(out=y_early[:, r, :], in_=acc[:])
-                nc.sync.dma_start(out=out_rows[:, r, :], in_=y_early[:, r, :])
-            else:
-                nc.scalar.copy(out=y_late[:, :, 0, :], in_=acc[:].rearrange("p (c m) -> p c m", m=CHUNK))
-                nc.sync.dma_start(out=out_rows[:, r, :].rearrange("p (c m) -> p c m", m=CHUNK), in_=y_late[:, :, 0, :])
+            nc.scalar.copy(out=y[:, :, r, :], in_=acc[:].rearrange("p (c m) -> p c m", m=CHUNK))
+            nc.sync.dma_start(out=out_rows[:, r, :].rearrange("p (c m) -> p c m", m=CHUNK), in_=y[:, :, r, :])
 
         last = PACK - 1
         firsts = []
         j0 = 0
         for width in FIRST_PIECES:
-            firsts.append((j0, double(expert(0, j0, width), 0, width, f"first{j0}")))
+            firsts.append((j0, double(expert(0, j0, width), 0, keep.tile([P, width], F32, name=f"first{j0}"))))
             j0 = j0 + width
-        second = double(expert(1, 0, J), 0, J, "second")
-        late_accs = {r: expert(r, 0, J) for r in (2, last)}
-        late_heads = {r: double(late_accs[r], 0, HALF, f"head{r}") for r in (2, last)}
+        second = double(expert(1, 0, J), 0, keep.tile([P, J], F32, name="second"))
+        acc2 = expert(2, 0, J)
+        head2 = double(acc2, 0, keep.tile([P, HEAD2], F32, name="head2"))
+        acc3 = expert(last, 0, J)
+        head3 = double(acc3, 0, keep.tile([P, HALF], F32, name="head3"))
         nc.gpsimd.tensor_scalar(out=ct_half[:], in0=ct[:], scalar1=0.5, scalar2=None, op0=MULT)
-        dealt = {(r, g): deal_old(r, g) for r, g in ON_TENSOR}
+        dealt = {(r, g): deal_old(r, g) for r in range(2) for g in range(PASSES)}
         nc.sync.dma_start(out=olds[last][:], in_=old_rows[:, last, :])
+        grouped = [keep.tile([P, T], BF16, name=f"grouped{r}", align_bytes=64) for r in range(last)]
+        flats = {
+            (0, 0): keep.tile([P, PACK, P], BF16, name="flat00"),
+            (0, 1): late.tile([P, PACK, P], BF16, name="flat01", offset=4096),
+            (1, 0): keep.tile([P, PACK, P], BF16, name="flat10"),
+            (1, 1): late.tile([P, PACK, P], BF16, name="flat11", offset=0),
+        }
+        pages = {(r, g): keep.tile([P, PACK, P], F32, name=f"page{r}{g}") for r, g in ((2, 0), (last, 0), (last, 1))}
+        pages[2, 1] = late.tile([P, PACK, P], F32, name="page21", offset=1024)
+
+        def front(r):
+            for g in range(PASSES):
+                bank = turn_adding_on_tensor(r, g, dealt[r, g])
+                weigh_on_scalar(bank, g, grouped[r][:, g * PASS : (g + 1) * PASS], flats[r, g])
 
         for j0, doubled in firsts:
             scatter(0, j0, doubled)
-        grouped0 = front(0)
+        front(0)
         scatter(1, 0, second)
-        grouped1 = front(1)
-        scatter(2, 0, late_heads[2])
-        rest = double(late_accs[2], HALF, HALF, "flat0_1")
-        back(0, grouped0)
-        scatter(2, HALF, rest)
-        grouped2 = front(2)
-        scatter(last, 0, late_heads[last])
-        rest = double(late_accs[last], HALF, HALF, "flat1_1")
-        back(1, grouped1)
-        nc.scalar.copy(out=rounded[:, :, 0:2], in_=y_early[:].rearrange("p r m -> p m r"))
-        scatter(last, HALF, rest)
+        front(1)
+        scatter(2, 0, head2)
+        rest2 = double(acc2, HEAD2, late.tile([P, J - HEAD2], F32, name="rest2", offset=4096))
+        back(0, grouped[0])
+        scatter(2, HEAD2, rest2)
+        banks = [turn_adding_on_vector(2, g, pages[2, g]) for g in range(PASSES)]
+        scatter(last, 0, head3)
+        rest3 = double(acc3, HALF, late.tile([P, HALF], F32, name="rest3", offset=512))
+        for g in range(PASSES):
+            weigh_on_vector(banks[g], g, grouped[2][:, g * PASS : (g + 1) * PASS])
+        back(1, grouped[1])
+        back(2, grouped[2])
+        scatter(last, HALF, rest3)
 
-        banks = [turn_adding_on_vector(last, g) for g in range(PASSES)]
-        back(2, grouped2)
+        banks = [turn_adding_on_vector(last, g, pages[last, g]) for g in range(PASSES)]
         tails = [keep.tile([P, PASS], BF16, name=f"tail{g}", align_bytes=64) for g in range(PASSES)]
         for g in range(PASSES):
             weigh_on_vector(banks[g], g, tails[g][:, 0:PASS])
@@ -256,8 +254,11 @@ def tile_moe_expert_page_to_keys_pl_kernel(
 
         def finish(c):
             cols = slice(c * CHUNK, (c + 1) * CHUNK)
-            nc.scalar.copy(out=y_late[:, c, 1, :], in_=accs[c][:, 0:CHUNK])
-            nc.vector.tensor_copy(out=rounded[:, cols, 2:4], in_=y_late[:, c, :, :].rearrange("p r m -> p m r"))
+            nc.scalar.copy(out=y[:, c, last, :], in_=accs[c][:, 0:CHUNK])
+            nc.vector.tensor_copy(
+                out=rounded[:, cols, :].rearrange("p (b e) r -> p b r e", e=2),
+                in_=y[:, c, :, :].rearrange("p r (b e) -> p b r e", e=2),
+            )
 
         def planes(m0, m1):
             nc.vector.quantize_mx(
@@ -268,8 +269,8 @@ def tile_moe_expert_page_to_keys_pl_kernel(
 
         def store(h):
             cols = slice(h * HALF, (h + 1) * HALF)
-            nc.scalar.dma_start(
-                out=out_rows[:, last, cols].rearrange("p (c m) -> p c m", m=CHUNK), in_=y_late[:, 2 * h : 2 * h + 2, 1, :]
+            nc.sync.dma_start(
+                out=out_rows[:, last, cols].rearrange("p (c m) -> p c m", m=CHUNK), in_=y[:, 2 * h : 2 * h + 2, last, :]
             )
             nc.sync.dma_start(
                 out=words_out[:, h * HALF * PACK : (h + 1) * HALF * PACK].bitcast(I32), in_=y_codes[:, cols].bitcast(I32)
@@ -285,7 +286,7 @@ def tile_moe_expert_page_to_keys_pl_kernel(
         store(0)
         store(1)
         for quad in range(4):
-            queue = nc.sync if quad % 2 == 0 else nc.scalar
+            queue = nc.scalar if quad % 2 == 0 else nc.sync
             queue.dma_start(
                 out=out_2[0, 4 * quad : 4 * quad + 4, :].bitcast(I32),
                 in_=y_scales[32 * quad : 32 * quad + 4, :].bitcast(I32),

@@ -60,7 +60,7 @@ def tile_moe_expert_page_to_keys_pl_kernel(
         ct_half = keep.tile([P, PASSES, PACK], F32, name="ct_half")
         ident = keep.tile([P, P], F32, name="ident")
         olds = [loads.tile([P, T], F32, name=f"old{r}", offset=at) for r, at in enumerate((0, 5024, 9216, 0))]
-        windows = [keep.tile([P, T], F32, name="window0"), loads.tile([P, T], F32, name="window1", offset=17280)]
+        windows = [keep.tile([P, T], F32, name=f"window{i}") for i in range(2)]
         y = keep.tile([P, M // CHUNK, PACK, CHUNK], F32, name="y")
         rounded = keep.tile([P, M, PACK], BF16, name="rounded", align_bytes=64)
         y_scales = keep.tile([P, M], U8, name="y_scales", align_bytes=64)
@@ -73,14 +73,13 @@ def tile_moe_expert_page_to_keys_pl_kernel(
         nc.sync.dma_start(out=w_raw[:], in_=w_words.rearrange("z p n t -> p z (n t)").bitcast(I32))
         load_scales(nc, nc.sync, xs, xt_scales, range(4))
         make_identity(nc, ident[:])
-        nc.vector.memset(windows[0][:], 0.0)
+        for window in windows:
+            nc.vector.memset(window[:], 0.0)
 
-        nc.vector.tensor_copy(
-            out=ws[:].rearrange("p r z q -> p z q r"),
-            in_=ws_raw[:].rearrange("p z (q r) -> p z q r", r=PACK),
-        )
+        ws_cols = ws_raw[:].rearrange("p z (q r) -> p r z q", r=PACK)
         w_cols = w_raw[:].rearrange("p z (q a e) -> p a z q e", a=2, e=2)
         for a in range(2):
+            nc.vector.tensor_copy(out=ws[:, 2 * a : 2 * a + 2], in_=ws_cols[:, 2 * a : 2 * a + 2])
             nc.vector.tensor_copy(out=w_dealt[a][:].rearrange("p e z q -> p z q e"), in_=w_cols[:, a])
 
         old_rows = old.rearrange("(p r) t -> p r t", r=PACK)
@@ -88,7 +87,6 @@ def tile_moe_expert_page_to_keys_pl_kernel(
         nc.sync.dma_start(out=ct[:], in_=ct1.rearrange("(g p r) o -> p g (r o)", g=PASSES, r=PACK))
         nc.sync.dma_start(out=olds[1][:], in_=old_rows[:, 1, :])
         nc.gpsimd.memset(ks[:].rearrange("p z c -> p (z c)").bitcast(I32), 0)
-        nc.gpsimd.memset(windows[1][:], 0.0)
         nc.sync.dma_start(out=kw[:].bitcast(I32), in_=ky_words.rearrange("z p c -> p z c").bitcast(I32))
         load_scales(nc, nc.sync, ks, ky_scales, range(4))
         nc.sync.dma_start(out=olds[2][:], in_=old_rows[:, 2, :])
@@ -200,9 +198,8 @@ def tile_moe_expert_page_to_keys_pl_kernel(
         acc2 = expert(2, 0, J)
         head2 = double(acc2, 0, keep.tile([P, HEAD2], F32, name="head2"))
         acc3 = expert(last, 0, J)
-        head3 = double(acc3, 0, keep.tile([P, HALF], F32, name="head3"))
         nc.gpsimd.tensor_scalar(out=ct_half[:], in0=ct[:], scalar1=0.5, scalar2=None, op0=MULT)
-        dealt = {(r, g): deal_old(r, g) for r in range(2) for g in range(PASSES)}
+        dealt = {(r, g): deal_old(r, g) for r in range(last) for g in range(PASSES)}
         nc.sync.dma_start(out=olds[last][:], in_=old_rows[:, last, :])
         grouped = [keep.tile([P, T], BF16, name=f"grouped{r}", align_bytes=64) for r in range(last)]
         flats = {
@@ -211,8 +208,7 @@ def tile_moe_expert_page_to_keys_pl_kernel(
             (1, 0): keep.tile([P, PACK, P], BF16, name="flat10"),
             (1, 1): late.tile([P, PACK, P], BF16, name="flat11", offset=0),
         }
-        pages = {(r, g): keep.tile([P, PACK, P], F32, name=f"page{r}{g}") for r, g in ((2, 0), (last, 0), (last, 1))}
-        pages[2, 1] = late.tile([P, PACK, P], F32, name="page21", offset=1024)
+        pages = [keep.tile([P, PACK, P], F32, name=f"page{g}") for g in range(PASSES)]
 
         def front(r):
             for g in range(PASSES):
@@ -226,18 +222,19 @@ def tile_moe_expert_page_to_keys_pl_kernel(
         front(1)
         scatter(2, 0, head2)
         rest2 = double(acc2, HEAD2, late.tile([P, J - HEAD2], F32, name="rest2", offset=4096))
+        head3 = double(acc3, 0, late.tile([P, HEAD2], F32, name="head3", offset=4608))
         back(0, grouped[0])
         scatter(2, HEAD2, rest2)
-        banks = [turn_adding_on_vector(2, g, pages[2, g]) for g in range(PASSES)]
+        banks = [turn_adding_on_tensor(2, g, dealt[2, g]) for g in range(PASSES)]
         scatter(last, 0, head3)
-        rest3 = double(acc3, HALF, late.tile([P, HALF], F32, name="rest3", offset=512))
+        rest3 = double(acc3, HEAD2, late.tile([P, J - HEAD2], F32, name="rest3", offset=0))
         for g in range(PASSES):
             weigh_on_vector(banks[g], g, grouped[2][:, g * PASS : (g + 1) * PASS])
         back(1, grouped[1])
         back(2, grouped[2])
-        scatter(last, HALF, rest3)
+        scatter(last, HEAD2, rest3)
 
-        banks = [turn_adding_on_vector(last, g, pages[last, g]) for g in range(PASSES)]
+        banks = [turn_adding_on_vector(last, g, pages[g]) for g in range(PASSES)]
         tails = [keep.tile([P, PASS], BF16, name=f"tail{g}", align_bytes=64) for g in range(PASSES)]
         for g in range(PASSES):
             weigh_on_vector(banks[g], g, tails[g][:, 0:PASS])
@@ -252,10 +249,10 @@ def tile_moe_expert_page_to_keys_pl_kernel(
         y_codes = keep.tile([P, M], U32, name="y_codes", align_bytes=64)
         words_out = out_1[0].rearrange("p c t -> p (c t)")
 
-        def finish(c):
+        def finish(c, copy):
             cols = slice(c * CHUNK, (c + 1) * CHUNK)
             nc.scalar.copy(out=y[:, c, last, :], in_=accs[c][:, 0:CHUNK])
-            nc.vector.tensor_copy(
+            copy(
                 out=rounded[:, cols, :].rearrange("p (b e) r -> p b r e", e=2),
                 in_=y[:, c, :, :].rearrange("p r (b e) -> p b r e", e=2),
             )
@@ -276,13 +273,11 @@ def tile_moe_expert_page_to_keys_pl_kernel(
                 out=words_out[:, h * HALF * PACK : (h + 1) * HALF * PACK].bitcast(I32), in_=y_codes[:, cols].bitcast(I32)
             )
 
-        finish(0)
-        finish(1)
-        finish(2)
+        for c in range(3):
+            finish(c, nc.vector.tensor_copy)
+        finish(3, nc.scalar.copy)
         planes(0, HALF)
-        finish(3)
-        planes(HALF, HALF + CHUNK)
-        planes(HALF + CHUNK, M)
+        planes(HALF, M)
         store(0)
         store(1)
         for quad in range(4):

from contextlib import ExitStack

import concourse.mybir as mybir
from concourse.masks import make_identity

K, T, J, N, M = 1024, 1024, 512, 512, 512
FLOPS = 2 * K * N * J + 2 * T * N * M

F32 = mybir.dt.float32
BF16 = mybir.dt.bfloat16
I32 = mybir.dt.int32
U32 = mybir.dt.uint32
U16 = mybir.dt.uint16
U8 = mybir.dt.uint8
FP8X4 = mybir.dt.float8_e4m3fn_x4
FP4X4 = mybir.dt.float4_e2m1fn_x4
COPY = mybir.ActivationFunctionType.Copy
ADD = mybir.AluOpType.add
MULT = mybir.AluOpType.mult

P = 128
PACK = 4
PASS = P * PACK
PASSES = 2
FIRST_PIECES = (128, 384)
HEAD2 = 384
CHUNK = 128
HALF = 256


def load_scales(nc, queue, plane, scales, rows):
    for r in rows:
        queue.dma_start(
            out=plane[r:P:32, :, :].bitcast(I32),
            in_=scales[:, r:16:4, :].rearrange("z q c -> q z c").bitcast(I32),
        )


def tile_moe_expert_page_to_keys_pl_kernel(
    tc, xt_words, xt_scales, w_words, w_scales, old, ct1, ky_words, ky_scales, offs, out_0, out_1, out_2
):
    nc = tc.nc
    with ExitStack() as ctx:
        keep = ctx.enter_context(tc.tile_pool(name="keep", bufs=1))
        ring = ctx.enter_context(tc.tile_pool(name="ring", bufs=2))
        late = ctx.enter_context(tc.tile_pool(name="late", bufs=1))
        loads = ctx.enter_context(tc.tile_pool(name="loads", bufs=1))
        psum = ctx.enter_context(tc.psum_pool(name="psum", bufs=8))

        offsets = keep.tile([P, J // 16], U16, name="offsets")
        ws_raw = loads.tile([P, PASSES, N], U8, name="ws_raw", align_bytes=64, offset=4032)
        xs = keep.tile([P, PASSES, J], U8, name="xs", align_bytes=64)
        ks = loads.tile([P, PASSES, M], U8, name="ks", align_bytes=64, offset=15360)
        w_raw = loads.tile([P, PASSES, N], I32, name="w_raw", align_bytes=64, offset=13248)
        xw = keep.tile([P, PASSES, 2 * J], U8, name="xw", align_bytes=64)
        kw = loads.tile([P, PASSES, 2 * M], U8, name="kw", align_bytes=64, offset=13312)
        w_dealt = [keep.tile([P, 2, PASSES, P], I32, name=f"w_dealt{a}", align_bytes=64) for a in range(2)]
        ws = keep.tile([P, PACK, PASSES, P], U8, name="ws", align_bytes=64)
        ct = loads.tile([P, PASSES, PACK], F32, name="ct", offset=4096)
        ct_half = keep.tile([P, PASSES, PACK], F32, name="ct_half")
        ident = keep.tile([P, P], F32, name="ident")
        olds = [loads.tile([P, T], F32, name=f"old{r}", offset=at) for r, at in enumerate((0, 5024, 9216, 0))]
        windows = [keep.tile([P, T], F32, name=f"window{i}") for i in range(2)]
        y = keep.tile([P, M // CHUNK, PACK, CHUNK], F32, name="y")
        rounded = keep.tile([P, M, PACK], BF16, name="rounded", align_bytes=64)
        y_scales = keep.tile([P, M], U8, name="y_scales", align_bytes=64)

        nc.vector.memset(ws_raw[:].rearrange("p z c -> p (z c)").bitcast(I32), 0)
        nc.vector.memset(xs[:].rearrange("p z c -> p (z c)").bitcast(I32), 0)
        nc.sync.dma_start(offsets[:], offs)
        nc.sync.dma_start(out=xw[:].bitcast(I32), in_=xt_words.rearrange("z p c -> p z c").bitcast(I32))
        load_scales(nc, nc.sync, ws_raw, w_scales, range(4))
        nc.sync.dma_start(out=w_raw[:], in_=w_words.rearrange("z p n t -> p z (n t)").bitcast(I32))
        load_scales(nc, nc.sync, xs, xt_scales, range(4))
        make_identity(nc, ident[:])
        for window in windows:
            nc.vector.memset(window[:], 0.0)

        ws_cols = ws_raw[:].rearrange("p z (q r) -> p r z q", r=PACK)
        w_cols = w_raw[:].rearrange("p z (q a e) -> p a z q e", a=2, e=2)
        for a in range(2):
            nc.vector.tensor_copy(out=ws[:, 2 * a : 2 * a + 2], in_=ws_cols[:, 2 * a : 2 * a + 2])
            nc.vector.tensor_copy(out=w_dealt[a][:].rearrange("p e z q -> p z q e"), in_=w_cols[:, a])

        old_rows = old.rearrange("(p r) t -> p r t", r=PACK)
        nc.sync.dma_start(out=olds[0][:], in_=old_rows[:, 0, :])
        nc.sync.dma_start(out=ct[:], in_=ct1.rearrange("(g p r) o -> p g (r o)", g=PASSES, r=PACK))
        nc.sync.dma_start(out=olds[1][:], in_=old_rows[:, 1, :])
        nc.gpsimd.memset(ks[:].rearrange("p z c -> p (z c)").bitcast(I32), 0)
        nc.sync.dma_start(out=kw[:].bitcast(I32), in_=ky_words.rearrange("z p c -> p z c").bitcast(I32))
        load_scales(nc, nc.sync, ks, ky_scales, range(4))
        nc.sync.dma_start(out=olds[2][:], in_=old_rows[:, 2, :])

        def w_block(r, z):
            return w_dealt[r // 2][:, r % 2, z, :].bitcast(FP8X4)

        def expert(r, j0, width):
            acc = psum.tile([P, J], F32, name="bank", tag="bank")
            step = J if width == J else CHUNK
            for c in range(0, width, step):
                for z in range(PASSES):
                    nc.tensor.matmul_mx(
                        out=acc[:, c : c + step],
                        lhsT=w_block(r, z),
                        lhsT_scale=ws[:, r, z, :],
                        rhs=xw[:, z, 2 * (j0 + c) : 2 * (j0 + c + step)].bitcast(FP4X4),
                        rhs_scale=xs[:, z, j0 + c : j0 + c + step],
                        start=(z == 0),
                        stop=(z == PASSES - 1),
                    )
            return acc

        def double(acc, c0, doubled):
            nc.scalar.activation(out=doubled[:], in_=acc[:, c0 : c0 + doubled.shape[1]], func=COPY, scale=2.0)
            return doubled

        def scatter(r, j0, doubled):
            width = doubled.shape[1]
            window = windows[r % 2]
            nc.vector.tensor_copy(window[:].indirect(offsets[:, j0 // 16 : (j0 + width) // 16]), doubled[:])

        def deal_old(r, g):
            dealt = keep.tile([P, PACK, P], F32, name=f"old_dealt{r}_{g}")
            nc.scalar.copy(
                out=dealt[:].rearrange("p (a e) q -> p a q e", e=2),
                in_=olds[r][:, g * PASS : (g + 1) * PASS].rearrange("p (q a e) -> p a q e", a=2, e=2),
            )
            return dealt

        def turn_adding_on_tensor(r, g, dealt):
            bank = psum.tile([P, PACK, P], F32, name="bank", tag="bank")
            for s in range(PACK):
                nc.tensor.matmul(bank[:, s, :], dealt[:, s, :], ident[:], start=(s == 0), stop=False, is_transpose=True)
            for s in range(PACK):
                cols = windows[r % 2][:, g * PASS + s : (g + 1) * PASS : PACK]
                nc.tensor.matmul(bank[:, s, :], cols, ident[:], start=False, stop=(s == PACK - 1), is_transpose=True)
            return bank

        def turn_adding_on_vector(r, g, page):
            cols = slice(g * PASS, (g + 1) * PASS)
            nc.vector.tensor_tensor(
                out=page[:].rearrange("p (a e) q -> p a q e", e=2),
                in0=windows[r % 2][:, cols].rearrange("p (q a e) -> p a q e", a=2, e=2),
                in1=olds[r][:, cols].rearrange("p (q a e) -> p a q e", a=2, e=2),
                op=ADD,
            )
            bank = psum.tile([P, PACK, P], F32, name="bank", tag="bank")
            for s in range(PACK):
                nc.tensor.transpose(bank[:, s, :], page[:, s, :], ident[:])
            return bank

        def weigh_on_scalar(bank, g, grouped, flat):
            for s in range(PACK):
                nc.scalar.activation(out=flat[:, s, :], in_=bank[:, s, :], func=COPY, scale=ct_half[:, g, s : s + 1])
            nc.scalar.copy(
                out=grouped.rearrange("p (c i s) -> p c s i", i=4, s=PACK),
                in_=flat[:].rearrange("p s (c i) -> p c s i", i=4),
            )

        def weigh_on_vector(bank, g, grouped):
            nc.vector.tensor_tensor(
                out=grouped.rearrange("p (c e s) -> p c s e", e=2, s=PACK),
                in0=bank[:].rearrange("p s (c e) -> p c s e", e=2),
                in1=ct_half[:, g, :].unsqueeze(1).unsqueeze(3).to_broadcast([P, P // 2, PACK, 2]),
                op=MULT,
            )

        out_rows = out_0.rearrange("(p r) m -> p r m", r=PACK)

        def keys(codes, scales, g, acc, m0, width):
            nc.tensor.matmul_mx(
                out=acc,
                lhsT=codes.bitcast(FP8X4),
                lhsT_scale=scales,
                rhs=kw[:, g, 2 * m0 : 2 * (m0 + width)].bitcast(FP4X4),
                rhs_scale=ks[:, g, m0 : m0 + width],
                start=(g == 0),
                stop=(g == PASSES - 1),
            )

        def back(r, grouped):
            codes = ring.tile([P, PASSES * P], U32, name="codes", tag="codes", align_bytes=64)
            scales = ring.tile([P, PASSES * P], U8, name="scales", tag="scales", align_bytes=64)
            nc.vector.quantize_mx(out=codes[:].bitcast(FP8X4), scales=scales[:], in_=grouped[:])
            acc = psum.tile([P, M], F32, name="bank", tag="bank")
            for g in range(PASSES):
                keys(codes[:, g * P : (g + 1) * P], scales[:, g * P : (g + 1) * P], g, acc[:], 0, M)
            nc.scalar.copy(out=y[:, :, r, :], in_=acc[:].rearrange("p (c m) -> p c m", m=CHUNK))
            nc.sync.dma_start(out=out_rows[:, r, :].rearrange("p (c m) -> p c m", m=CHUNK), in_=y[:, :, r, :])

        last = PACK - 1
        firsts = []
        j0 = 0
        for width in FIRST_PIECES:
            firsts.append((j0, double(expert(0, j0, width), 0, keep.tile([P, width], F32, name=f"first{j0}"))))
            j0 = j0 + width
        second = double(expert(1, 0, J), 0, keep.tile([P, J], F32, name="second"))
        acc2 = expert(2, 0, J)
        head2 = double(acc2, 0, keep.tile([P, HEAD2], F32, name="head2"))
        acc3 = expert(last, 0, J)
        nc.gpsimd.tensor_scalar(out=ct_half[:], in0=ct[:], scalar1=0.5, scalar2=None, op0=MULT)
        dealt = {(r, g): deal_old(r, g) for r in range(last) for g in range(PASSES)}
        nc.sync.dma_start(out=olds[last][:], in_=old_rows[:, last, :])
        grouped = [keep.tile([P, T], BF16, name=f"grouped{r}", align_bytes=64) for r in range(last)]
        flats = {
            (0, 0): keep.tile([P, PACK, P], BF16, name="flat00"),
            (0, 1): late.tile([P, PACK, P], BF16, name="flat01", offset=4096),
            (1, 0): keep.tile([P, PACK, P], BF16, name="flat10"),
            (1, 1): late.tile([P, PACK, P], BF16, name="flat11", offset=0),
        }
        pages = [keep.tile([P, PACK, P], F32, name=f"page{g}") for g in range(PASSES)]

        def front(r):
            for g in range(PASSES):
                bank = turn_adding_on_tensor(r, g, dealt[r, g])
                weigh_on_scalar(bank, g, grouped[r][:, g * PASS : (g + 1) * PASS], flats[r, g])

        for j0, doubled in firsts:
            scatter(0, j0, doubled)
        front(0)
        scatter(1, 0, second)
        front(1)
        scatter(2, 0, head2)
        rest2 = double(acc2, HEAD2, late.tile([P, J - HEAD2], F32, name="rest2", offset=4096))
        head3 = double(acc3, 0, late.tile([P, HEAD2], F32, name="head3", offset=4608))
        back(0, grouped[0])
        scatter(2, HEAD2, rest2)
        banks = [turn_adding_on_tensor(2, g, dealt[2, g]) for g in range(PASSES)]
        scatter(last, 0, head3)
        rest3 = double(acc3, HEAD2, late.tile([P, J - HEAD2], F32, name="rest3", offset=0))
        for g in range(PASSES):
            weigh_on_vector(banks[g], g, grouped[2][:, g * PASS : (g + 1) * PASS])
        back(1, grouped[1])
        back(2, grouped[2])
        scatter(last, HEAD2, rest3)

        banks = [turn_adding_on_vector(last, g, pages[g]) for g in range(PASSES)]
        tails = [keep.tile([P, PASS], BF16, name=f"tail{g}", align_bytes=64) for g in range(PASSES)]
        for g in range(PASSES):
            weigh_on_vector(banks[g], g, tails[g][:, 0:PASS])
        accs = [psum.tile([P, M], F32, name="bank", tag="bank") for c in range(M // CHUNK)]
        for g in range(PASSES):
            codes = keep.tile([P, P], U32, name=f"last_codes{g}", align_bytes=64)
            scales = keep.tile([P, P], U8, name=f"last_scales{g}", align_bytes=64)
            nc.vector.quantize_mx(out=codes[:].bitcast(FP8X4), scales=scales[:], in_=tails[g][:, 0:PASS])
            for c in range(M // CHUNK):
                keys(codes[:], scales[:], g, accs[c][:, 0:CHUNK], c * CHUNK, CHUNK)

        y_codes = keep.tile([P, M], U32, name="y_codes", align_bytes=64)
        words_out = out_1[0].rearrange("p c t -> p (c t)")

        def finish(c, copy):
            cols = slice(c * CHUNK, (c + 1) * CHUNK)
            nc.scalar.copy(out=y[:, c, last, :], in_=accs[c][:, 0:CHUNK])
            copy(
                out=rounded[:, cols, :].rearrange("p (b e) r -> p b r e", e=2),
                in_=y[:, c, :, :].rearrange("p r (b e) -> p b r e", e=2),
            )

        def planes(m0, m1):
            nc.vector.quantize_mx(
                out=y_codes[:, m0:m1].bitcast(FP8X4),
                scales=y_scales[:, m0:m1],
                in_=rounded[:, m0:m1, :].rearrange("p m r -> p (m r)"),
            )

        def store(h):
            cols = slice(h * HALF, (h + 1) * HALF)
            nc.sync.dma_start(
                out=out_rows[:, last, cols].rearrange("p (c m) -> p c m", m=CHUNK), in_=y[:, 2 * h : 2 * h + 2, last, :]
            )
            nc.sync.dma_start(
                out=words_out[:, h * HALF * PACK : (h + 1) * HALF * PACK].bitcast(I32), in_=y_codes[:, cols].bitcast(I32)
            )

        for c in range(3):
            finish(c, nc.vector.tensor_copy)
        finish(3, nc.scalar.copy)
        planes(0, HALF)
        planes(HALF, M)
        store(0)
        store(1)
        for quad in range(4):
            queue = nc.scalar if quad % 2 == 0 else nc.sync
            queue.dma_start(
                out=out_2[0, 4 * quad : 4 * quad + 4, :].bitcast(I32),
                in_=y_scales[32 * quad : 32 * quad + 4, :].bitcast(I32),
            )
